import numpy as np
import ml_dtypes


def mxq(x, axis, fmt="e4m3"):
    dtype, down = {"e4m3": (ml_dtypes.float8_e4m3fn, 7), "e5m2": (ml_dtypes.float8_e5m2, 14)}[fmt]
    v = np.moveaxis(np.asarray(x, np.float32).astype(ml_dtypes.bfloat16).astype(np.float64), axis, -1)
    blocks = v.reshape(v.shape[:-1] + (-1, 32))
    amax = np.abs(blocks).max(-1, keepdims=True)
    byte = np.maximum(np.where(amax > 0, np.frexp(amax)[1] - 1 + 127, 0) - down, 1)
    scale = np.exp2(byte - 127.0)
    codes = (blocks / scale).astype(np.float32).astype(dtype).astype(np.float64)
    return np.moveaxis((codes * scale).reshape(v.shape), -1, axis)


WIDE = False


def mx_kscale(k):
    if not WIDE:
        return np.ones(k)
    levels = np.array([10, -10, 5, -5, 0])
    if k % 512:
        return np.exp2(np.random.permutation(np.resize(levels, k // 32))).repeat(32)
    a = np.empty((k // 512, 16))
    for p in range(k // 512):
        a[p, :8] = np.random.permutation(np.resize(levels, 8))
        for g in range(8):
            far = levels[np.abs(levels - a[p, g]) >= 10]
            a[p, g + 8] = far[np.random.randint(len(far))]
    return np.exp2(a.ravel()).repeat(32)


def f64(x):
    return np.asarray(x).astype(np.float64)


def striped(idx):
    return np.tile(idx.reshape(-1, 16).T, (8, 1)).astype(np.uint16)


def unstriped(offs):
    return offs[:16].T.reshape(-1).astype(np.int64)


E2M1 = np.array([0.0, 0.5, 1.0, 1.5, 2.0, 3.0, 4.0, 6.0, -0.0, -0.5, -1.0, -1.5, -2.0, -3.0, -4.0, -6.0])


def pack_weight(w, fmt):
    k, n = w.shape
    w = f64(np.asarray(w, np.float32).astype(ml_dtypes.bfloat16)).reshape(k // 32, 32, n)
    amax = np.abs(w).max(1)
    if fmt == "e4m3":
        byte = np.frexp(amax)[1] - 1 + 127 - 7
    else:
        mant, ex = np.frexp(amax / 6.0)
        byte = np.where(mant > 0.5, ex, ex - 1) + 127
    byte = np.clip(np.where(amax > 0, byte, 1), 1, 254)
    scaled = (w * np.exp2(127.0 - byte)[:, None, :]).reshape(k, n).astype(np.float32)
    by_word = np.ascontiguousarray(scaled.reshape(k // 512, 128, 4, n).transpose(0, 1, 3, 2))
    if fmt == "e4m3":
        words = by_word.astype(ml_dtypes.float8_e4m3fn).view(np.uint8)
    else:
        c = by_word.astype(ml_dtypes.float4_e2m1fn).view(np.uint8) & 0xF
        words = (c[..., 0::2] | (c[..., 1::2] << 4)).reshape(k // 512, 128, 2 * n)
    return np.ascontiguousarray(words), np.ascontiguousarray(byte.astype(np.uint8).reshape(k // 512, 16, n))


def unpack_weight(words, scales, fmt):
    g, _, n = scales.shape
    words = np.ascontiguousarray(words).reshape(g, 128, n, -1)
    if fmt == "e4m3":
        vals = words.view(ml_dtypes.float8_e4m3fn).astype(np.float64)
    else:
        nib = np.empty((g, 128, n, 4), np.uint8)
        nib[..., 0::2] = words & 0xF
        nib[..., 1::2] = words >> 4
        vals = E2M1[nib]
    vals = vals * np.repeat(np.exp2(scales.astype(np.float64) - 127.0), 8, axis=1)[..., None]
    return vals.transpose(0, 1, 3, 2).reshape(g * 512, n)


def gelu(v):
    return 0.5 * v * (1.0 + np.tanh(np.sqrt(2.0 / np.pi) * (v + 0.044715 * v**3)))


def striped8(idx):
    return np.concatenate([v.reshape(-1, 16).T for v in idx]).astype(np.uint16)


def unstriped8(offs):
    return np.stack([offs[16 * g:16 * g + 16].T.reshape(-1) for g in range(8)]).astype(np.int64)


def heads(h, wgt, idx8):
    r = np.arange(h.shape[0])
    return wgt[r // 4 % 128] * h[r[:, None], idx8[r % 512 // 64]]


K, T, S, P, H, N = 1024, 4096, 1024, 512, 1024, 768


def setup_inputs():
    n = np.random.standard_normal
    s = mx_kscale(K)[:, None]
    u = mx_kscale(H)[:, None]
    tab_words, tab_scales = pack_weight(n((K, T)) * s, "e4m3")
    w4_words, w4_scales = pack_weight(1.3 * n((H, N)) / np.sqrt(H) / u, "e2m1")
    return {
        "tab_words": tab_words,
        "tab_scales": tab_scales,
        "offs": striped(np.random.permutation(T)[:S]),
        "w1": (0.35 * n((K, H)) / np.sqrt(K) / s).astype(np.float32),
        "tide": np.random.uniform(-1.0, 1.0, (H, S)).astype(np.float32),
        "gain": (2.0 * np.exp(0.3 * n(H)) * u[:, 0]).astype(np.float32),
        "offs2": striped8(np.stack([np.random.permutation(S)[:P] for _ in range(8)])),
        "offs3": striped8(np.stack([np.random.permutation(S)[:P] for _ in range(8)])),
        "wga": np.repeat(np.random.uniform(0.5, 2.0, (8, P)), 16, axis=0).astype(np.float32),
        "wgb": np.repeat(np.random.uniform(0.5, 2.0, (8, P)), 16, axis=0).astype(np.float32),
        "w4_words": w4_words,
        "w4_scales": w4_scales,
    }


def reference(tab_words, tab_scales, offs, w1, tide, gain, offs2, offs3, wga, wgb, w4_words, w4_scales):
    v = unpack_weight(tab_words, tab_scales, "e4m3")[:, unstriped(offs)]
    d = mxq(f64(w1), 0, "e4m3").T @ v
    h = f64(gain)[:, None] * (d * np.cos(d + f64(tide)))
    xa = heads(h, f64(wga), unstriped8(offs2))
    xb = heads(h, f64(wgb), unstriped8(offs3))
    x = xa + xb
    w4 = unpack_weight(w4_words, w4_scales, "e2m1")
    y = w4.T @ mxq(x, 0, "e4m3")
    return np.tanh(y)

@@ -1,0 +1,262 @@
+import math
+from contextlib import ExitStack
+
+import concourse.mybir as mybir
+
+K, T, S, M, H, N = 1024, 4096, 1024, 512, 1024, 768
+FLOPS = 2 * K * H * S + 2 * H * N * M
+
+F32 = mybir.dt.float32
+BF16 = mybir.dt.bfloat16
+I32 = mybir.dt.int32
+U32 = mybir.dt.uint32
+U16 = mybir.dt.uint16
+U8 = mybir.dt.uint8
+FP8X4 = mybir.dt.float8_e4m3fn_x4
+FP4X4 = mybir.dt.float4_e2m1fn_x4
+ACT = mybir.ActivationFunctionType
+ALU = mybir.AluOpType
+
+P = 128
+PACK = 4
+PASS = P * PACK
+BANK = 512
+SLICES = H // P
+HALF = M // 2
+N_TILES = N // P
+
+
+def tile_list_tuna_dive_scores_kernel(
+    tc, tab_words, tab_scales, offs, w1, tide, gain, offs2, offs3, wga, wgb, w4_words, w4_scales, out
+):
+    nc = tc.nc
+    with ExitStack() as ctx:
+        keep = ctx.enter_context(tc.tile_pool(name="keep", bufs=1))
+        ring = ctx.enter_context(tc.tile_pool(name="ring", bufs=2))
+        psum = ctx.enter_context(tc.psum_pool(name="psum", bufs=8))
+
+        list1 = keep.tile([P, S // 16], U16, name="list1")
+        list2 = keep.tile([P, M // 16], U16, name="list2")
+        list3 = keep.tile([P, M // 16], U16, name="list3")
+        words = [keep.tile([P, T], U32, name=f"words{a}") for a in range(2)]
+        tab_planes = keep.tile([P, T], U8, name="tab_planes")
+        v_codes = [keep.tile([P, S], U32, name=f"v_codes{a}", align_bytes=64) for a in range(2)]
+        v_planes = keep.tile([P, S], U8, name="v_planes", align_bytes=64)
+        w1_raw = {(b, a): keep.tile([P, PACK, PASS], F32, name=f"w1_raw{b}{a}") for b in range(2) for a in range(2)}
+        tides = [keep.tile([P, S], F32, name=f"tide{s}") for s in range(SLICES)]
+        gains = keep.tile([P, 2, PACK], F32, name="gains")
+        wa = keep.tile([P, M], F32, name="wa")
+        wb = keep.tile([P, M], F32, name="wb")
+        w4_codes = keep.tile([P, 2, 2 * N], U8, name="w4_codes", align_bytes=64)
+        w4_planes = keep.tile([P, 2, N], U8, name="w4_planes", align_bytes=64)
+        xa = keep.tile([P, PACK, M], F32, name="xa")
+        xb = keep.tile([P, PACK, M], F32, name="xb")
+
+        def load_w1(b, a):
+            rows = w1[a * PASS : (a + 1) * PASS, b * PASS : (b + 1) * PASS]
+            nc.sync.dma_start(out=w1_raw[b, a][:], in_=rows.rearrange("(p t) c -> p t c", t=PACK))
+
+        tide_rows = tide.rearrange("(b p i) j -> b i p j", p=P, i=PACK)
+
+        def load_tide(s):
+            nc.sync.dma_start(out=tides[s][:], in_=tide_rows[s // PACK, s % PACK])
+
+        nc.vector.memset(tab_planes[:].bitcast(I32), 0)
+        nc.vector.memset(w4_planes[:].rearrange("p a n -> p (a n)").bitcast(I32), 0)
+
+        nc.sync.dma_start(list1[:], offs)
+
+        def load_words(a):
+            nc.sync.dma_start(
+                out=words[a][:].bitcast(I32), in_=tab_words[a].rearrange("p t i -> p (t i)").bitcast(I32)
+            )
+
+        load_words(0)
+        for q in range(4):
+            nc.sync.dma_start(
+                out=tab_planes[32 * q : 32 * q + 8, :].bitcast(I32),
+                in_=tab_scales[:, 4 * q : 4 * q + 4, :].bitcast(I32),
+            )
+        load_words(1)
+        load_w1(0, 0)
+        load_w1(0, 1)
+        load_tide(0)
+        load_tide(1)
+        nc.sync.dma_start(out=gains[:], in_=gain.rearrange("(b p i) -> p b i", p=P, i=PACK))
+        nc.sync.dma_start(list2[:], offs2)
+        nc.sync.dma_start(list3[:], offs3)
+        load_tide(2)
+        nc.sync.dma_start(out=wa[:], in_=wga)
+        nc.sync.dma_start(out=wb[:], in_=wgb)
+        load_w1(1, 0)
+        load_tide(3)
+        load_w1(1, 1)
+        for s in range(4, SLICES):
+            load_tide(s)
+        nc.sync.dma_start(out=w4_codes[:].bitcast(I32), in_=w4_words.rearrange("a p c -> p a c").bitcast(I32))
+        for q in range(4):
+            nc.sync.dma_start(
+                out=w4_planes[32 * q : 32 * q + 4, :, :].bitcast(I32),
+                in_=w4_scales[:, 4 * q : 4 * q + 4, :].rearrange("a r n -> r a n").bitcast(I32),
+            )
+
+        nc.vector.tensor_copy(v_codes[0][:], words[0][:].indirect(list1[:]))
+        nc.vector.tensor_copy(v_planes[:], tab_planes[:].indirect(list1[:]))
+        nc.vector.tensor_copy(v_codes[1][:], words[1][:].indirect(list1[:]))
+
+        w1_bf, w1_codes, w1_planes = {}, {}, {}
+
+        def round_w1(b, a, u, copy):
+            t = ring.tile([P, 2 * PASS], BF16, name="w1_bf", tag="w1_bf", bufs=4, align_bytes=64)
+            copy(
+                t[:].rearrange("p (i m t) -> p m t i", i=2, t=PACK),
+                w1_raw[b, a][:].rearrange("p t (m i) -> p m t i", i=PACK)[:, :, :, 2 * u : 2 * u + 2],
+            )
+            w1_bf[b, a, u] = t
+
+        def quantise_w1(b, a, u):
+            codes = keep.tile([P, 2 * P], U32, name=f"w1_codes{b}{a}{u}", align_bytes=64)
+            planes = keep.tile([P, 2 * P], U8, name=f"w1_planes{b}{a}{u}", align_bytes=64)
+            nc.vector.quantize_mx(out=codes[:].bitcast(FP8X4), scales=planes[:], in_=w1_bf[b, a, u][:])
+            w1_codes[b, a, u] = codes
+            w1_planes[b, a, u] = planes
+
+        for a in range(2):
+            round_w1(0, a, 0, nc.vector.tensor_copy)
+            round_w1(0, a, 1, nc.scalar.copy)
+            quantise_w1(0, a, 0)
+            quantise_w1(0, a, 1)
+
+        d, c, h = {}, {}, {}
+
+        def first_product(s):
+            b, i = divmod(s, PACK)
+            u, e = divmod(i, 2)
+            cols = slice(e * P, (e + 1) * P)
+            for j in range(2):
+                bank = psum.tile([P, BANK], F32, name="bank", tag="bank")
+                for a in range(2):
+                    nc.tensor.matmul_mx(
+                        out=bank[:],
+                        lhsT=w1_codes[b, a, u][:, cols].bitcast(FP8X4),
+                        lhsT_scale=w1_planes[b, a, u][:, cols],
+                        rhs=v_codes[a][:, j * BANK : (j + 1) * BANK].bitcast(FP8X4),
+                        rhs_scale=v_planes[4 * a : P, j * BANK : (j + 1) * BANK],
+                        start=(a == 0),
+                        stop=(a == 1),
+                    )
+                d[s, j] = bank
+
+        def cosine(s):
+            for j in range(2):
+                z = ring.tile([P, BANK], F32, name="z", tag="z", bufs=6)
+                nc.vector.tensor_tensor(z[:], d[s, j][:], tides[s][:, j * BANK : (j + 1) * BANK], ALU.add)
+                c[s, j] = z
+            for j in range(2):
+                nc.scalar.activation(c[s, j][:], c[s, j][:], ACT.Abs)
+            for j in range(2):
+                nc.scalar.activation(c[s, j][:], c[s, j][:], ACT.Sin, bias=math.pi / 2, scale=-1.0)
+
+        def features(s):
+            b, i = divmod(s, PACK)
+            t = ring.tile([P, S], F32, name="h", tag="h")
+            for j in range(2):
+                nc.vector.scalar_tensor_tensor(
+                    t[:, j * BANK : (j + 1) * BANK], d[s, j][:], gains[:, b, i : i + 1], c[s, j][:], ALU.mult, ALU.mult
+                )
+            h[s] = t
+
+        def picks(s, lo, hi):
+            i = s % PACK
+            nc.vector.tensor_tensor(xa[:, i, lo:hi], h[s][:].indirect(list2[:, lo // 16 : hi // 16]), wa[:, lo:hi], ALU.mult)
+            nc.vector.tensor_tensor(xb[:, i, lo:hi], h[s][:].indirect(list3[:, lo // 16 : hi // 16]), wb[:, lo:hi], ALU.mult)
+
+        x_bf, x_codes, x_planes = {}, {}, {}
+
+        def add_picks(b, g):
+            t = ring.tile([P, HALF * PACK], BF16, name="x_bf", tag="x_bf", align_bytes=64)
+            cols = slice(g * HALF, (g + 1) * HALF)
+            nc.vector.tensor_tensor(
+                t[:].rearrange("p (c e i) -> p c i e", e=2, i=PACK),
+                xa[:, :, cols].rearrange("p i (c e) -> p c i e", e=2),
+                xb[:, :, cols].rearrange("p i (c e) -> p c i e", e=2),
+                ALU.add,
+            )
+            x_bf[b, g] = t
+
+        def quantise_x(b, g):
+            codes = keep.tile([P, HALF], U32, name=f"x_codes{b}{g}", align_bytes=64)
+            planes = keep.tile([P, HALF], U8, name=f"x_planes{b}{g}", align_bytes=64)
+            nc.vector.quantize_mx(out=codes[:].bitcast(FP8X4), scales=planes[:], in_=x_bf[b, g][:])
+            x_codes[b, g] = codes
+            x_planes[b, g] = planes
+
+        y = {}
+
+        def second_product(n, g, b):
+            if b == 0:
+                y[n, g] = psum.tile([P, BANK], F32, name="bank", tag="bank")
+            nc.tensor.matmul_mx(
+                out=y[n, g][:, 0:HALF],
+                lhsT=w4_codes[:, b, 2 * n * P : 2 * (n + 1) * P].bitcast(FP4X4),
+                lhsT_scale=w4_planes[:, b, n * P : (n + 1) * P],
+                rhs=x_codes[b, g][:].bitcast(FP8X4),
+                rhs_scale=x_planes[b, g][:],
+                start=(b == 0),
+                stop=(b == 1),
+            )
+
+        out_tiles = out.rearrange("(n p) m -> p n m", p=P)
+
+        def scores(g):
+            for pair in range(N_TILES // 2):
+                t = keep.tile([P, 2, HALF], F32, name=f"scores{g}{pair}")
+                for e in range(2):
+                    n = 2 * pair + e
+                    second_product(n, g, 1)
+                    nc.scalar.activation(t[:, e, :], y[n, g][:, 0:HALF], ACT.Tanh)
+                nc.sync.dma_start(out=out_tiles[:, 2 * pair : 2 * pair + 2, g * HALF : (g + 1) * HALF], in_=t[:])
+
+        late_w1 = [(1, a, u) for u in range(2) for a in range(2)]
+        first_product(0)
+        first_product(1)
+        cosine(0)
+        cosine(1)
+        first_product(2)
+        for s in range(SLICES - 1):
+            features(s)
+            if s + 3 < SLICES and s + 3 != PACK:
+                first_product(s + 3)
+            if s == 1:
+                quantise_w1(*late_w1[0])
+                quantise_w1(*late_w1[1])
+                first_product(PACK)
+            if s == 2:
+                quantise_w1(*late_w1[2])
+                quantise_w1(*late_w1[3])
+            if s == PACK:
+                add_picks(0, 0)
+                add_picks(0, 1)
+            if s + 2 < SLICES:
+                cosine(s + 2)
+            if s < 2:
+                round_w1(*late_w1[2 * s], nc.scalar.copy)
+                round_w1(*late_w1[2 * s + 1], nc.scalar.copy)
+            if s == PACK:
+                quantise_x(0, 0)
+                quantise_x(0, 1)
+            picks(s, 0, M)
+        last = SLICES - 1
+        for n in range(N_TILES):
+            second_product(n, 0, 0)
+        features(last)
+        picks(last, 0, HALF)
+        add_picks(1, 0)
+        picks(last, HALF, M)
+        quantise_x(1, 0)
+        scores(0)
+        add_picks(1, 1)
+        for n in range(N_TILES):
+            second_product(n, 1, 0)
+        quantise_x(1, 1)
+        scores(1)

@@ -22,7 +22,7 @@ PACK = 4
 PASS = P * PACK
 BANK = 512
 SLICES = H // P
-HALF = M // 2
+PIECES = ((0, 256), (256, 384), (384, 512))
 N_TILES = N // P
 
 
@@ -49,8 +49,7 @@ def tile_list_tuna_dive_scores_kernel(
         wb = keep.tile([P, M], F32, name="wb")
         w4_codes = keep.tile([P, 2, 2 * N], U8, name="w4_codes", align_bytes=64)
         w4_planes = keep.tile([P, 2, N], U8, name="w4_planes", align_bytes=64)
-        xa = keep.tile([P, PACK, M], F32, name="xa")
-        xb = keep.tile([P, PACK, M], F32, name="xb")
+        x_rows = [keep.tile([P, PACK, M], BF16, name=f"x_rows{b}") for b in range(2)]
 
         def load_w1(b, a):
             rows = w1[a * PASS : (a + 1) * PASS, b * PASS : (b + 1) * PASS]
@@ -63,6 +62,10 @@ def tile_list_tuna_dive_scores_kernel(
 
         nc.vector.memset(tab_planes[:].bitcast(I32), 0)
         nc.vector.memset(w4_planes[:].rearrange("p a n -> p (a n)").bitcast(I32), 0)
+
+        warm = keep.tile([P, 1], F32, name="warm")
+        nc.gpsimd.memset(warm[:], 0.0)
+        nc.scalar.activation(warm[:], warm[:], ACT.Silu)
 
         nc.sync.dma_start(list1[:], offs)
 
@@ -150,7 +153,7 @@ def tile_list_tuna_dive_scores_kernel(
         def cosine(s):
             for j in range(2):
                 z = ring.tile([P, BANK], F32, name="z", tag="z", bufs=6)
-                nc.vector.tensor_tensor(z[:], d[s, j][:], tides[s][:, j * BANK : (j + 1) * BANK], ALU.add)
+                nc.vector.tensor_tensor(z[:], tides[s][:, j * BANK : (j + 1) * BANK], d[s, j][:], ALU.add)
                 c[s, j] = z
             for j in range(2):
                 nc.scalar.activation(c[s, j][:], c[s, j][:], ACT.Abs)
@@ -162,60 +165,66 @@ def tile_list_tuna_dive_scores_kernel(
             t = ring.tile([P, S], F32, name="h", tag="h")
             for j in range(2):
                 nc.vector.scalar_tensor_tensor(
-                    t[:, j * BANK : (j + 1) * BANK], d[s, j][:], gains[:, b, i : i + 1], c[s, j][:], ALU.mult, ALU.mult
+                    t[:, j * BANK : (j + 1) * BANK], c[s, j][:], gains[:, b, i : i + 1], d[s, j][:], ALU.mult, ALU.mult
                 )
             h[s] = t
 
         def picks(s, lo, hi):
-            i = s % PACK
-            nc.vector.tensor_tensor(xa[:, i, lo:hi], h[s][:].indirect(list2[:, lo // 16 : hi // 16]), wa[:, lo:hi], ALU.mult)
-            nc.vector.tensor_tensor(xb[:, i, lo:hi], h[s][:].indirect(list3[:, lo // 16 : hi // 16]), wb[:, lo:hi], ALU.mult)
+            xa = ring.tile([P, hi - lo], F32, name="xa", tag="xa")
+            xb = ring.tile([P, hi - lo], F32, name="xb", tag="xb")
+            nc.vector.tensor_tensor(xa[:], h[s][:].indirect(list2[:, lo // 16 : hi // 16]), wa[:, lo:hi], ALU.mult)
+            nc.vector.tensor_tensor(xb[:], h[s][:].indirect(list3[:, lo // 16 : hi // 16]), wb[:, lo:hi], ALU.mult)
+            return xa, xb
 
-        x_bf, x_codes, x_planes = {}, {}, {}
+        def add_picks(s, lo, hi, pair, engine):
+            b, i = divmod(s, PACK)
+            engine.tensor_tensor(x_rows[b][:, i, lo:hi], pair[0][:], pair[1][:], ALU.add)
 
-        def add_picks(b, g):
-            t = ring.tile([P, HALF * PACK], BF16, name="x_bf", tag="x_bf", align_bytes=64)
-            cols = slice(g * HALF, (g + 1) * HALF)
-            nc.vector.tensor_tensor(
-                t[:].rearrange("p (c e i) -> p c i e", e=2, i=PACK),
-                xa[:, :, cols].rearrange("p i (c e) -> p c i e", e=2),
-                xb[:, :, cols].rearrange("p i (c e) -> p c i e", e=2),
-                ALU.add,
+        x_bf = {}
+        x_codes = [keep.tile([P, M], U32, name=f"x_codes{b}", align_bytes=64) for b in range(2)]
+        x_planes = [keep.tile([P, M], U8, name=f"x_planes{b}", align_bytes=64) for b in range(2)]
+
+        def interleave(b, lo, hi, copy):
+            t = keep.tile([P, (hi - lo) * PACK], BF16, name=f"x_bf{b}_{lo}", align_bytes=64)
+            copy(
+                t[:].rearrange("p (c e i) -> p c i e", e=4, i=PACK),
+                x_rows[b][:, :, lo:hi].rearrange("p i (c e) -> p c i e", e=4),
             )
-            x_bf[b, g] = t
+            x_bf[b, lo] = t
 
-        def quantise_x(b, g):
-            codes = keep.tile([P, HALF], U32, name=f"x_codes{b}{g}", align_bytes=64)
-            planes = keep.tile([P, HALF], U8, name=f"x_planes{b}{g}", align_bytes=64)
-            nc.vector.quantize_mx(out=codes[:].bitcast(FP8X4), scales=planes[:], in_=x_bf[b, g][:])
-            x_codes[b, g] = codes
-            x_planes[b, g] = planes
+        def quantise_x(b, lo, hi):
+            nc.vector.quantize_mx(
+                out=x_codes[b][:, lo:hi].bitcast(FP8X4), scales=x_planes[b][:, lo:hi], in_=x_bf[b, lo][:]
+            )
 
         y = {}
 
-        def second_product(n, g, b):
+        def bank_tiles(lo, hi):
+            per_bank = BANK // (hi - lo)
+            return [range(n0, min(n0 + per_bank, N_TILES)) for n0 in range(0, N_TILES, per_bank)]
+
+        def second_product(lo, hi, tiles, b):
             if b == 0:
-                y[n, g] = psum.tile([P, BANK], F32, name="bank", tag="bank")
-            nc.tensor.matmul_mx(
-                out=y[n, g][:, 0:HALF],
-                lhsT=w4_codes[:, b, 2 * n * P : 2 * (n + 1) * P].bitcast(FP4X4),
-                lhsT_scale=w4_planes[:, b, n * P : (n + 1) * P],
-                rhs=x_codes[b, g][:].bitcast(FP8X4),
-                rhs_scale=x_planes[b, g][:],
-                start=(b == 0),
-                stop=(b == 1),
-            )
+                y[lo, tiles[0]] = psum.tile([P, len(tiles), hi - lo], F32, name="bank", tag="bank")
+            for n in tiles:
+                nc.tensor.matmul_mx(
+                    out=y[lo, tiles[0]][:, n - tiles[0], :],
+                    lhsT=w4_codes[:, b, 2 * n * P : 2 * (n + 1) * P].bitcast(FP4X4),
+                    lhsT_scale=w4_planes[:, b, n * P : (n + 1) * P],
+                    rhs=x_codes[b][:, lo:hi].bitcast(FP8X4),
+                    rhs_scale=x_planes[b][:, lo:hi],
+                    start=(b == 0 and n == tiles[0]),
+                    stop=(b == 1 and n == tiles[-1]),
+                )
 
         out_tiles = out.rearrange("(n p) m -> p n m", p=P)
 
-        def scores(g):
-            for pair in range(N_TILES // 2):
-                t = keep.tile([P, 2, HALF], F32, name=f"scores{g}{pair}")
-                for e in range(2):
-                    n = 2 * pair + e
-                    second_product(n, g, 1)
-                    nc.scalar.activation(t[:, e, :], y[n, g][:, 0:HALF], ACT.Tanh)
-                nc.sync.dma_start(out=out_tiles[:, 2 * pair : 2 * pair + 2, g * HALF : (g + 1) * HALF], in_=t[:])
+        def scores(lo, hi):
+            for tiles in bank_tiles(lo, hi):
+                t = keep.tile([P, len(tiles), hi - lo], F32, name=f"scores{lo}_{tiles[0]}")
+                second_product(lo, hi, tiles, 1)
+                nc.scalar.activation(t[:], y[lo, tiles[0]][:], ACT.Tanh)
+                nc.sync.dma_start(out=out_tiles[:, tiles[0] : tiles[-1] + 1, lo:hi], in_=t[:])
 
         late_w1 = [(1, a, u) for u in range(2) for a in range(2)]
         first_product(0)
@@ -227,6 +236,8 @@ def tile_list_tuna_dive_scores_kernel(
             features(s)
             if s + 3 < SLICES and s + 3 != PACK:
                 first_product(s + 3)
+            if s + 2 < SLICES:
+                cosine(s + 2)
             if s == 1:
                 quantise_w1(*late_w1[0])
                 quantise_w1(*late_w1[1])
@@ -234,29 +245,20 @@ def tile_list_tuna_dive_scores_kernel(
             if s == 2:
                 quantise_w1(*late_w1[2])
                 quantise_w1(*late_w1[3])
-            if s == PACK:
-                add_picks(0, 0)
-                add_picks(0, 1)
-            if s + 2 < SLICES:
-                cosine(s + 2)
             if s < 2:
                 round_w1(*late_w1[2 * s], nc.scalar.copy)
                 round_w1(*late_w1[2 * s + 1], nc.scalar.copy)
             if s == PACK:
-                quantise_x(0, 0)
-                quantise_x(0, 1)
-            picks(s, 0, M)
+                interleave(0, 0, M, nc.scalar.copy)
+            add_picks(s, 0, M, picks(s, 0, M), nc.gpsimd)
         last = SLICES - 1
-        for n in range(N_TILES):
-            second_product(n, 0, 0)
         features(last)
-        picks(last, 0, HALF)
-        add_picks(1, 0)
-        picks(last, HALF, M)
-        quantise_x(1, 0)
-        scores(0)
-        add_picks(1, 1)
-        for n in range(N_TILES):
-            second_product(n, 1, 0)
-        quantise_x(1, 1)
-        scores(1)
+        quantise_x(0, 0, M)
+        for lo, hi in PIECES:
+            for tiles in bank_tiles(lo, hi):
+                second_product(lo, hi, tiles, 0)
+        for lo, hi in PIECES:
+            add_picks(last, lo, hi, picks(last, lo, hi), nc.vector)
+            interleave(1, lo, hi, nc.vector.tensor_copy)
+            quantise_x(1, lo, hi)
+            scores(lo, hi)

@@ -2,6 +2,7 @@ import math
 from contextlib import ExitStack
 
 import concourse.mybir as mybir
+from concourse.masks import make_identity
 
 K, T, S, M, H, N = 1024, 4096, 1024, 512, 1024, 768
 FLOPS = 2 * K * H * S + 2 * H * N * M
@@ -22,6 +23,8 @@ PACK = 4
 PASS = P * PACK
 BANK = 512
 SLICES = H // P
+FIRST_TURNED = 3
+BANKS = {"d_first": 3, "d_second": 1, "turned_sum": 2, "cosine": 2}
 PIECES = ((0, 256), (256, 384), (384, 512))
 N_TILES = N // P
 
@@ -33,7 +36,7 @@ def tile_list_tuna_dive_scores_kernel(
     with ExitStack() as ctx:
         keep = ctx.enter_context(tc.tile_pool(name="keep", bufs=1))
         ring = ctx.enter_context(tc.tile_pool(name="ring", bufs=2))
-        psum = ctx.enter_context(tc.psum_pool(name="psum", bufs=8))
+        psum = ctx.enter_context(tc.psum_pool(name="psum", bufs=1))
 
         list1 = keep.tile([P, S // 16], U16, name="list1")
         list2 = keep.tile([P, M // 16], U16, name="list2")
@@ -43,13 +46,19 @@ def tile_list_tuna_dive_scores_kernel(
         v_codes = [keep.tile([P, S], U32, name=f"v_codes{a}", align_bytes=64) for a in range(2)]
         v_planes = keep.tile([P, S], U8, name="v_planes", align_bytes=64)
         w1_raw = {(b, a): keep.tile([P, PACK, PASS], F32, name=f"w1_raw{b}{a}") for b in range(2) for a in range(2)}
-        tides = [keep.tile([P, S], F32, name=f"tide{s}") for s in range(SLICES)]
+        tides = [keep.tile([P, S], F32, name=f"tide{s}", tag=f"tide{s}") for s in range(SLICES)]
         gains = keep.tile([P, 2, PACK], F32, name="gains")
         wa = keep.tile([P, M], F32, name="wa")
         wb = keep.tile([P, M], F32, name="wb")
         w4_codes = keep.tile([P, 2, 2 * N], U8, name="w4_codes", align_bytes=64)
         w4_planes = keep.tile([P, 2, N], U8, name="w4_planes", align_bytes=64)
         x_rows = [keep.tile([P, PACK, M], BF16, name=f"x_rows{b}") for b in range(2)]
+
+        identity = keep.tile([P, P], F32, name="identity")
+        make_identity(nc, identity[:])
+
+        def new_bank(role, shape=(P, BANK)):
+            return psum.tile(list(shape), F32, name=role, tag=role, bufs=BANKS[role])
 
         def load_w1(b, a):
             rows = w1[a * PASS : (a + 1) * PASS, b * PASS : (b + 1) * PASS]
@@ -88,13 +97,12 @@ def tile_list_tuna_dive_scores_kernel(
         nc.sync.dma_start(out=gains[:], in_=gain.rearrange("(b p i) -> p b i", p=P, i=PACK))
         nc.sync.dma_start(list2[:], offs2)
         nc.sync.dma_start(list3[:], offs3)
-        load_tide(2)
         nc.sync.dma_start(out=wa[:], in_=wga)
         nc.sync.dma_start(out=wb[:], in_=wgb)
         load_w1(1, 0)
-        load_tide(3)
+        load_tide(2)
         load_w1(1, 1)
-        for s in range(4, SLICES):
+        for s in range(3, SLICES):
             load_tide(s)
         nc.sync.dma_start(out=w4_codes[:].bitcast(I32), in_=w4_words.rearrange("a p c -> p a c").bitcast(I32))
         for q in range(4):
@@ -132,53 +140,88 @@ def tile_list_tuna_dive_scores_kernel(
 
         d, c, h = {}, {}, {}
 
-        def first_product(s):
+        def first_product(s, j):
             b, i = divmod(s, PACK)
             u, e = divmod(i, 2)
             cols = slice(e * P, (e + 1) * P)
-            for j in range(2):
-                bank = psum.tile([P, BANK], F32, name="bank", tag="bank")
-                for a in range(2):
-                    nc.tensor.matmul_mx(
-                        out=bank[:],
-                        lhsT=w1_codes[b, a, u][:, cols].bitcast(FP8X4),
-                        lhsT_scale=w1_planes[b, a, u][:, cols],
-                        rhs=v_codes[a][:, j * BANK : (j + 1) * BANK].bitcast(FP8X4),
-                        rhs_scale=v_planes[4 * a : P, j * BANK : (j + 1) * BANK],
-                        start=(a == 0),
-                        stop=(a == 1),
-                    )
-                d[s, j] = bank
+            bank = new_bank("d_first" if j == 0 else "d_second" if turned(s, j) else "turned_sum" if s == 2 else "cosine")
+            for a in range(2):
+                nc.tensor.matmul_mx(
+                    out=bank[:],
+                    lhsT=w1_codes[b, a, u][:, cols].bitcast(FP8X4),
+                    lhsT_scale=w1_planes[b, a, u][:, cols],
+                    rhs=v_codes[a][:, j * BANK : (j + 1) * BANK].bitcast(FP8X4),
+                    rhs_scale=v_planes[4 * a : P, j * BANK : (j + 1) * BANK],
+                    start=(a == 0),
+                    stop=(a == 1),
+                )
+            d[s, j] = bank
 
-        def cosine(s):
-            for j in range(2):
-                z = ring.tile([P, BANK], F32, name="z", tag="z", bufs=6)
-                nc.vector.tensor_tensor(z[:], tides[s][:, j * BANK : (j + 1) * BANK], d[s, j][:], ALU.add)
-                c[s, j] = z
-            for j in range(2):
-                nc.scalar.activation(c[s, j][:], c[s, j][:], ACT.Abs)
-            for j in range(2):
-                nc.scalar.activation(c[s, j][:], c[s, j][:], ACT.Sin, bias=math.pi / 2, scale=-1.0)
+        z = {}
+
+        def turned(s, j):
+            return j == 1 and s >= FIRST_TURNED
+
+        def add_tide(s, j):
+            z[s, j] = ring.tile([P, BANK], F32, name="c", tag="c", bufs=6)
+            c[s, j] = z[s, j]
+            nc.vector.tensor_tensor(z[s, j][:], tides[s][:, j * BANK : (j + 1) * BANK], d[s, j][:], ALU.add)
+
+        def hold_d(s):
+            held = ring.tile([P, BANK], F32, name="held", tag="held", bufs=4)
+            nc.scalar.copy(held[:], d[s, 1][:])
+            d[s, 1] = held
+
+        def add_tide_turned(s):
+            z[s, 1] = new_bank("turned_sum")
+            c[s, 1] = ring.tile([P, BANK], F32, name="c", tag="c", bufs=6)
+            for part, source in enumerate((tides[s][:, BANK:S], d[s, 1][:])):
+                for k in range(BANK // P):
+                    nc.tensor.matmul(
+                        z[s, 1][:, k * P : (k + 1) * P],
+                        source[:, k * P : (k + 1) * P],
+                        identity[:],
+                        start=(part == 0 and k == 0),
+                        stop=(part == 1 and k == BANK // P - 1),
+                        is_transpose=True,
+                    )
+
+        def magnitude(s, j):
+            nc.scalar.activation(c[s, j][:], z[s, j][:], ACT.Abs)
+
+        def cosine(s, j):
+            nc.scalar.activation(c[s, j][:], c[s, j][:], ACT.Sin, bias=math.pi / 2, scale=-1.0)
+
+        def turn_back(s):
+            bank = new_bank("cosine")
+            for k in range(BANK // P):
+                nc.tensor.transpose(bank[:, k * P : (k + 1) * P], c[s, 1][:, k * P : (k + 1) * P], identity[:])
+            c[s, 1] = bank
 
         def features(s):
             b, i = divmod(s, PACK)
             t = ring.tile([P, S], F32, name="h", tag="h")
             for j in range(2):
+                in_sbuf, in_psum = (d[s, j], c[s, j]) if turned(s, j) else (c[s, j], d[s, j])
                 nc.vector.scalar_tensor_tensor(
-                    t[:, j * BANK : (j + 1) * BANK], c[s, j][:], gains[:, b, i : i + 1], d[s, j][:], ALU.mult, ALU.mult
+                    t[:, j * BANK : (j + 1) * BANK], in_sbuf[:], gains[:, b, i : i + 1], in_psum[:], ALU.mult, ALU.mult
                 )
             h[s] = t
 
-        def picks(s, lo, hi):
-            xa = ring.tile([P, hi - lo], F32, name="xa", tag="xa")
-            xb = ring.tile([P, hi - lo], F32, name="xb", tag="xb")
-            nc.vector.tensor_tensor(xa[:], h[s][:].indirect(list2[:, lo // 16 : hi // 16]), wa[:, lo:hi], ALU.mult)
-            nc.vector.tensor_tensor(xb[:], h[s][:].indirect(list3[:, lo // 16 : hi // 16]), wb[:, lo:hi], ALU.mult)
-            return xa, xb
+        picked = {}
 
-        def add_picks(s, lo, hi, pair, engine):
+        def pick(s, side, lo, hi):
+            offsets, weights = ((list2, wa), (list3, wb))[side]
+            if side == 0 and s + 2 < SLICES:
+                t = keep.tile([P, hi - lo], F32, name="picked", tag=f"tide{s + 2}")
+            else:
+                t = ring.tile([P, hi - lo], F32, name="picked", tag="picked", bufs=4)
+            nc.vector.tensor_tensor(t[:], h[s][:].indirect(offsets[:, lo // 16 : hi // 16]), weights[:, lo:hi], ALU.mult)
+            picked[s, side, lo] = t
+
+        def add_picks(s, lo, hi, engine):
             b, i = divmod(s, PACK)
-            engine.tensor_tensor(x_rows[b][:, i, lo:hi], pair[0][:], pair[1][:], ALU.add)
+            engine.tensor_tensor(x_rows[b][:, i, lo:hi], picked[s, 0, lo][:], picked[s, 1, lo][:], ALU.add)
 
         x_bf = {}
         x_codes = [keep.tile([P, M], U32, name=f"x_codes{b}", align_bytes=64) for b in range(2)]
@@ -198,6 +241,7 @@ def tile_list_tuna_dive_scores_kernel(
             )
 
         y = {}
+        roles = [role for role, count in BANKS.items() for k in range(count)]
 
         def bank_tiles(lo, hi):
             per_bank = BANK // (hi - lo)
@@ -205,7 +249,7 @@ def tile_list_tuna_dive_scores_kernel(
 
         def second_product(lo, hi, tiles, b):
             if b == 0:
-                y[lo, tiles[0]] = psum.tile([P, len(tiles), hi - lo], F32, name="bank", tag="bank")
+                y[lo, tiles[0]] = new_bank(roles[len(y)], (P, len(tiles), hi - lo))
             for n in tiles:
                 nc.tensor.matmul_mx(
                     out=y[lo, tiles[0]][:, n - tiles[0], :],
@@ -227,38 +271,84 @@ def tile_list_tuna_dive_scores_kernel(
                 nc.sync.dma_start(out=out_tiles[:, tiles[0] : tiles[-1] + 1, lo:hi], in_=t[:])
 
         late_w1 = [(1, a, u) for u in range(2) for a in range(2)]
-        first_product(0)
-        first_product(1)
-        cosine(0)
-        cosine(1)
-        first_product(2)
+        for s in range(2):
+            for j in range(2):
+                first_product(s, j)
+        for s in range(2):
+            for step in (add_tide, magnitude, cosine):
+                for j in range(2):
+                    step(s, j)
+        first_product(2, 0)
+        first_product(2, 1)
+        first_product(3, 1)
         for s in range(SLICES - 1):
             features(s)
-            if s + 3 < SLICES and s + 3 != PACK:
-                first_product(s + 3)
+            if s + 3 < SLICES:
+                if s + 3 != PACK:
+                    first_product(s + 3, 0)
+                if turned(s + 3, 1) and s + 3 != PACK:
+                    hold_d(s + 3)
+                    add_tide_turned(s + 3)
+            if s == 0:
+                round_w1(*late_w1[0], nc.scalar.copy)
+                round_w1(*late_w1[1], nc.scalar.copy)
             if s + 2 < SLICES:
-                cosine(s + 2)
+                add_tide(s + 2, 0)
+                if not turned(s + 2, 1):
+                    add_tide(s + 2, 1)
+                magnitude(s + 2, 1)
+                magnitude(s + 2, 0)
+                cosine(s + 2, 1)
+                cosine(s + 2, 0)
+                if turned(s + 2, 1):
+                    turn_back(s + 2)
             if s == 1:
-                quantise_w1(*late_w1[0])
-                quantise_w1(*late_w1[1])
-                first_product(PACK)
-            if s == 2:
-                quantise_w1(*late_w1[2])
-                quantise_w1(*late_w1[3])
-            if s < 2:
-                round_w1(*late_w1[2 * s], nc.scalar.copy)
-                round_w1(*late_w1[2 * s + 1], nc.scalar.copy)
-            if s == PACK:
-                interleave(0, 0, M, nc.scalar.copy)
-            add_picks(s, 0, M, picks(s, 0, M), nc.gpsimd)
+                round_w1(*late_w1[2], nc.scalar.copy)
+                round_w1(*late_w1[3], nc.scalar.copy)
+            if s in (1, 2):
+                quantise_w1(*late_w1[2 * s - 2])
+                quantise_w1(*late_w1[2 * s - 1])
+            if s == 1:
+                first_product(PACK, 1)
+                first_product(PACK, 0)
+                hold_d(PACK)
+                add_tide_turned(PACK)
+            if s >= 1 and s + 4 < SLICES:
+                first_product(s + 4, 1)
+            if s == SLICES - 3:
+                interleave(0, 0, M // 2, nc.scalar.copy)
+                interleave(0, M // 2, M, nc.scalar.copy)
+            pick(s, 0, 0, M)
+            pick(s, 1, 0, M)
+            add_picks(s, 0, M, nc.gpsimd)
         last = SLICES - 1
-        features(last)
-        quantise_x(0, 0, M)
-        for lo, hi in PIECES:
+        first, second, third = PIECES
+
+        def open_sums(lo, hi):
             for tiles in bank_tiles(lo, hi):
                 second_product(lo, hi, tiles, 0)
-        for lo, hi in PIECES:
-            add_picks(last, lo, hi, picks(last, lo, hi), nc.vector)
-            interleave(1, lo, hi, nc.vector.tensor_copy)
-            quantise_x(1, lo, hi)
-            scores(lo, hi)
+
+        features(last)
+        quantise_x(0, 0, M // 2)
+        open_sums(*first)
+        pick(last, 0, *first)
+        pick(last, 1, *first)
+        quantise_x(0, M // 2, M)
+        open_sums(*second)
+        open_sums(*third)
+        add_picks(last, *first, nc.vector)
+        pick(last, 0, *second)
+        interleave(1, *first, nc.vector.tensor_copy)
+        pick(last, 1, *second)
+        quantise_x(1, *first)
+        scores(*first)
+        add_picks(last, *second, nc.vector)
+        pick(last, 0, *third)
+        interleave(1, *second, nc.vector.tensor_copy)
+        pick(last, 1, *third)
+        quantise_x(1, *second)
+        scores(*second)
+        add_picks(last, *third, nc.vector)
+        interleave(1, *third, nc.vector.tensor_copy)
+        quantise_x(1, *third)
+        scores(*third)

@@ -21,12 +21,14 @@ ALU = mybir.AluOpType
 P = 128
 PACK = 4
 PASS = P * PACK
+PASSES = 2
+QUADRANTS = 4
 BANK = 512
 SLICES = H // P
-FIRST_TURNED = 3
-BANKS = {"d_first": 3, "d_second": 1, "turned_sum": 2, "cosine": 2}
-PIECES = ((0, 256), (256, 384), (384, 512))
 N_TILES = N // P
+FIRST_TURNED = 3
+BANKS = {"turned_sum": 2, "d_second": 1, "d_first": 3, "cosine": 2}
+PIECES = ((0, 256), (256, 384), (384, 512))
 
 
 def tile_list_tuna_dive_scores_kernel(
@@ -41,24 +43,32 @@ def tile_list_tuna_dive_scores_kernel(
         list1 = keep.tile([P, S // 16], U16, name="list1")
         list2 = keep.tile([P, M // 16], U16, name="list2")
         list3 = keep.tile([P, M // 16], U16, name="list3")
-        words = [keep.tile([P, T], U32, name=f"words{a}") for a in range(2)]
+        words = [keep.tile([P, T], U32, name=f"words{a}") for a in range(PASSES)]
         tab_planes = keep.tile([P, T], U8, name="tab_planes")
-        v_codes = [keep.tile([P, S], U32, name=f"v_codes{a}", align_bytes=64) for a in range(2)]
+        v_codes = [keep.tile([P, S], U32, name=f"v_codes{a}", align_bytes=64) for a in range(PASSES)]
         v_planes = keep.tile([P, S], U8, name="v_planes", align_bytes=64)
-        w1_raw = {(b, a): keep.tile([P, PACK, PASS], F32, name=f"w1_raw{b}{a}") for b in range(2) for a in range(2)}
+        w1_raw = {
+            (b, a): keep.tile([P, PACK, PASS], F32, name=f"w1_raw{b}{a}") for b in range(PASSES) for a in range(PASSES)
+        }
         tides = [keep.tile([P, S], F32, name=f"tide{s}", tag=f"tide{s}") for s in range(SLICES)]
-        gains = keep.tile([P, 2, PACK], F32, name="gains")
+        gains = keep.tile([P, PASSES, PACK], F32, name="gains")
         wa = keep.tile([P, M], F32, name="wa")
         wb = keep.tile([P, M], F32, name="wb")
-        w4_codes = keep.tile([P, 2, 2 * N], U8, name="w4_codes", align_bytes=64)
-        w4_planes = keep.tile([P, 2, N], U8, name="w4_planes", align_bytes=64)
-        x_rows = [keep.tile([P, PACK, M], BF16, name=f"x_rows{b}") for b in range(2)]
+        w4_codes = keep.tile([P, PASSES, 2 * N], U8, name="w4_codes", align_bytes=64)
+        w4_planes = keep.tile([P, PASSES, N], U8, name="w4_planes", align_bytes=64)
+        x_rows = [keep.tile([P, PACK, M], BF16, name=f"x_rows{b}") for b in range(PASSES)]
 
         identity = keep.tile([P, P], F32, name="identity")
         make_identity(nc, identity[:])
 
         def new_bank(role, shape=(P, BANK)):
             return psum.tile(list(shape), F32, name=role, tag=role, bufs=BANKS[role])
+
+
+        def load_words(a):
+            nc.sync.dma_start(
+                out=words[a][:].bitcast(I32), in_=tab_words[a].rearrange("p t i -> p (t i)").bitcast(I32)
+            )
 
         def load_w1(b, a):
             rows = w1[a * PASS : (a + 1) * PASS, b * PASS : (b + 1) * PASS]
@@ -77,16 +87,10 @@ def tile_list_tuna_dive_scores_kernel(
         nc.scalar.activation(warm[:], warm[:], ACT.Silu)
 
         nc.sync.dma_start(list1[:], offs)
-
-        def load_words(a):
-            nc.sync.dma_start(
-                out=words[a][:].bitcast(I32), in_=tab_words[a].rearrange("p t i -> p (t i)").bitcast(I32)
-            )
-
         load_words(0)
-        for q in range(4):
+        for q in range(QUADRANTS):
             nc.sync.dma_start(
-                out=tab_planes[32 * q : 32 * q + 8, :].bitcast(I32),
+                out=tab_planes[32 * q : 32 * q + 4 * PASSES, :].bitcast(I32),
                 in_=tab_scales[:, 4 * q : 4 * q + 4, :].bitcast(I32),
             )
         load_words(1)
@@ -97,33 +101,35 @@ def tile_list_tuna_dive_scores_kernel(
         nc.sync.dma_start(out=gains[:], in_=gain.rearrange("(b p i) -> p b i", p=P, i=PACK))
         nc.sync.dma_start(list2[:], offs2)
         nc.sync.dma_start(list3[:], offs3)
+        load_tide(2)
         nc.sync.dma_start(out=wa[:], in_=wga)
         nc.sync.dma_start(out=wb[:], in_=wgb)
         load_w1(1, 0)
-        load_tide(2)
         load_w1(1, 1)
         for s in range(3, SLICES):
             load_tide(s)
         nc.sync.dma_start(out=w4_codes[:].bitcast(I32), in_=w4_words.rearrange("a p c -> p a c").bitcast(I32))
-        for q in range(4):
+        for q in range(QUADRANTS):
             nc.sync.dma_start(
                 out=w4_planes[32 * q : 32 * q + 4, :, :].bitcast(I32),
                 in_=w4_scales[:, 4 * q : 4 * q + 4, :].rearrange("a r n -> r a n").bitcast(I32),
             )
 
+
         nc.vector.tensor_copy(v_codes[0][:], words[0][:].indirect(list1[:]))
         nc.vector.tensor_copy(v_planes[:], tab_planes[:].indirect(list1[:]))
         nc.vector.tensor_copy(v_codes[1][:], words[1][:].indirect(list1[:]))
 
+
         w1_bf, w1_codes, w1_planes = {}, {}, {}
 
         def round_w1(b, a, u, copy):
-            t = ring.tile([P, 2 * PASS], BF16, name="w1_bf", tag="w1_bf", bufs=4, align_bytes=64)
+            rounded = ring.tile([P, 2 * PASS], BF16, name="w1_bf", tag="w1_bf", bufs=4, align_bytes=64)
             copy(
-                t[:].rearrange("p (i m t) -> p m t i", i=2, t=PACK),
+                rounded[:].rearrange("p (i m t) -> p m t i", i=2, t=PACK),
                 w1_raw[b, a][:].rearrange("p t (m i) -> p m t i", i=PACK)[:, :, :, 2 * u : 2 * u + 2],
             )
-            w1_bf[b, a, u] = t
+            w1_bf[b, a, u] = rounded
 
         def quantise_w1(b, a, u):
             codes = keep.tile([P, 2 * P], U32, name=f"w1_codes{b}{a}{u}", align_bytes=64)
@@ -132,20 +138,31 @@ def tile_list_tuna_dive_scores_kernel(
             w1_codes[b, a, u] = codes
             w1_planes[b, a, u] = planes
 
-        for a in range(2):
+        for a in range(PASSES):
             round_w1(0, a, 0, nc.vector.tensor_copy)
             round_w1(0, a, 1, nc.scalar.copy)
             quantise_w1(0, a, 0)
             quantise_w1(0, a, 1)
 
-        d, c, h = {}, {}, {}
+
+        d, z, c, h = {}, {}, {}, {}
+
+        def turned(s, j):
+            return j == 1 and s >= FIRST_TURNED
+
+        def d_role(s, j):
+            if j == 0:
+                return "d_first"
+            if turned(s, j):
+                return "d_second"
+            return "cosine" if s < BANKS["cosine"] else "turned_sum"
 
         def first_product(s, j):
             b, i = divmod(s, PACK)
             u, e = divmod(i, 2)
             cols = slice(e * P, (e + 1) * P)
-            bank = new_bank("d_first" if j == 0 else "d_second" if turned(s, j) else "turned_sum" if s == 2 else "cosine")
-            for a in range(2):
+            bank = new_bank(d_role(s, j))
+            for a in range(PASSES):
                 nc.tensor.matmul_mx(
                     out=bank[:],
                     lhsT=w1_codes[b, a, u][:, cols].bitcast(FP8X4),
@@ -153,29 +170,25 @@ def tile_list_tuna_dive_scores_kernel(
                     rhs=v_codes[a][:, j * BANK : (j + 1) * BANK].bitcast(FP8X4),
                     rhs_scale=v_planes[4 * a : P, j * BANK : (j + 1) * BANK],
                     start=(a == 0),
-                    stop=(a == 1),
+                    stop=(a == PASSES - 1),
                 )
             d[s, j] = bank
 
-        z = {}
-
-        def turned(s, j):
-            return j == 1 and s >= FIRST_TURNED
+        def new_cosine_tile():
+            return ring.tile([P, BANK], F32, name="c", tag="c", bufs=6)
 
         def add_tide(s, j):
-            z[s, j] = ring.tile([P, BANK], F32, name="c", tag="c", bufs=6)
+            z[s, j] = new_cosine_tile()
             c[s, j] = z[s, j]
             nc.vector.tensor_tensor(z[s, j][:], tides[s][:, j * BANK : (j + 1) * BANK], d[s, j][:], ALU.add)
 
-        def hold_d(s):
+        def add_tide_turned(s):
             held = ring.tile([P, BANK], F32, name="held", tag="held", bufs=4)
             nc.scalar.copy(held[:], d[s, 1][:])
             d[s, 1] = held
-
-        def add_tide_turned(s):
             z[s, 1] = new_bank("turned_sum")
-            c[s, 1] = ring.tile([P, BANK], F32, name="c", tag="c", bufs=6)
-            for part, source in enumerate((tides[s][:, BANK:S], d[s, 1][:])):
+            c[s, 1] = new_cosine_tile()
+            for part, source in enumerate((tides[s][:, BANK:S], held[:])):
                 for k in range(BANK // P):
                     nc.tensor.matmul(
                         z[s, 1][:, k * P : (k + 1) * P],
@@ -200,40 +213,42 @@ def tile_list_tuna_dive_scores_kernel(
 
         def features(s):
             b, i = divmod(s, PACK)
-            t = ring.tile([P, S], F32, name="h", tag="h")
+            h[s] = ring.tile([P, S], F32, name="h", tag="h")
             for j in range(2):
                 in_sbuf, in_psum = (d[s, j], c[s, j]) if turned(s, j) else (c[s, j], d[s, j])
                 nc.vector.scalar_tensor_tensor(
-                    t[:, j * BANK : (j + 1) * BANK], in_sbuf[:], gains[:, b, i : i + 1], in_psum[:], ALU.mult, ALU.mult
+                    h[s][:, j * BANK : (j + 1) * BANK], in_sbuf[:], gains[:, b, i : i + 1], in_psum[:], ALU.mult, ALU.mult
                 )
-            h[s] = t
 
         picked = {}
 
         def pick(s, side, lo, hi):
             offsets, weights = ((list2, wa), (list3, wb))[side]
             if side == 0 and s + 2 < SLICES:
-                t = keep.tile([P, hi - lo], F32, name="picked", tag=f"tide{s + 2}")
+                result = keep.tile([P, hi - lo], F32, name="picked", tag=f"tide{s + 2}")
             else:
-                t = ring.tile([P, hi - lo], F32, name="picked", tag="picked", bufs=4)
-            nc.vector.tensor_tensor(t[:], h[s][:].indirect(offsets[:, lo // 16 : hi // 16]), weights[:, lo:hi], ALU.mult)
-            picked[s, side, lo] = t
+                result = ring.tile([P, hi - lo], F32, name="picked", tag="picked", bufs=4)
+            nc.vector.tensor_tensor(
+                result[:], h[s][:].indirect(offsets[:, lo // 16 : hi // 16]), weights[:, lo:hi], ALU.mult
+            )
+            picked[s, side, lo] = result
 
         def add_picks(s, lo, hi, engine):
             b, i = divmod(s, PACK)
             engine.tensor_tensor(x_rows[b][:, i, lo:hi], picked[s, 0, lo][:], picked[s, 1, lo][:], ALU.add)
 
+
         x_bf = {}
-        x_codes = [keep.tile([P, M], U32, name=f"x_codes{b}", align_bytes=64) for b in range(2)]
-        x_planes = [keep.tile([P, M], U8, name=f"x_planes{b}", align_bytes=64) for b in range(2)]
+        x_codes = [keep.tile([P, M], U32, name=f"x_codes{b}", align_bytes=64) for b in range(PASSES)]
+        x_planes = [keep.tile([P, M], U8, name=f"x_planes{b}", align_bytes=64) for b in range(PASSES)]
 
         def interleave(b, lo, hi, copy):
-            t = keep.tile([P, (hi - lo) * PACK], BF16, name=f"x_bf{b}_{lo}", align_bytes=64)
+            woven = keep.tile([P, (hi - lo) * PACK], BF16, name=f"x_bf{b}_{lo}", align_bytes=64)
             copy(
-                t[:].rearrange("p (c e i) -> p c i e", e=4, i=PACK),
+                woven[:].rearrange("p (c e i) -> p c i e", e=4, i=PACK),
                 x_rows[b][:, :, lo:hi].rearrange("p i (c e) -> p c i e", e=4),
             )
-            x_bf[b, lo] = t
+            x_bf[b, lo] = woven
 
         def quantise_x(b, lo, hi):
             nc.vector.quantize_mx(
@@ -244,7 +259,7 @@ def tile_list_tuna_dive_scores_kernel(
         roles = [role for role, count in BANKS.items() for k in range(count)]
 
         def bank_tiles(lo, hi):
-            per_bank = BANK // (hi - lo)
+            per_bank = 2 if hi == M else BANK // (hi - lo)
             return [range(n0, min(n0 + per_bank, N_TILES)) for n0 in range(0, N_TILES, per_bank)]
 
         def second_product(lo, hi, tiles, b):
@@ -258,40 +273,45 @@ def tile_list_tuna_dive_scores_kernel(
                     rhs=x_codes[b][:, lo:hi].bitcast(FP8X4),
                     rhs_scale=x_planes[b][:, lo:hi],
                     start=(b == 0 and n == tiles[0]),
-                    stop=(b == 1 and n == tiles[-1]),
+                    stop=(b == PASSES - 1 and n == tiles[-1]),
                 )
+
+        def open_sums(lo, hi):
+            for tiles in bank_tiles(lo, hi):
+                second_product(lo, hi, tiles, 0)
 
         out_tiles = out.rearrange("(n p) m -> p n m", p=P)
 
         def scores(lo, hi):
             for tiles in bank_tiles(lo, hi):
-                t = keep.tile([P, len(tiles), hi - lo], F32, name=f"scores{lo}_{tiles[0]}")
+                result = keep.tile([P, len(tiles), hi - lo], F32, name=f"scores{lo}_{tiles[0]}")
                 second_product(lo, hi, tiles, 1)
-                nc.scalar.activation(t[:], y[lo, tiles[0]][:], ACT.Tanh)
-                nc.sync.dma_start(out=out_tiles[:, tiles[0] : tiles[-1] + 1, lo:hi], in_=t[:])
+                nc.scalar.activation(result[:], y[lo, tiles[0]][:], ACT.Tanh)
+                queue = nc.scalar if hi == M and tiles[-1] == N_TILES - 1 else nc.sync
+                queue.dma_start(out=out_tiles[:, tiles[0] : tiles[-1] + 1, lo:hi], in_=result[:])
 
-        late_w1 = [(1, a, u) for u in range(2) for a in range(2)]
+
+        first, second, third = PIECES
+        last = SLICES - 1
         for s in range(2):
             for j in range(2):
                 first_product(s, j)
         for s in range(2):
-            for step in (add_tide, magnitude, cosine):
-                for j in range(2):
-                    step(s, j)
+            for j in range(2):
+                add_tide(s, j)
+                magnitude(s, j)
+                cosine(s, j)
         first_product(2, 0)
         first_product(2, 1)
         first_product(3, 1)
-        for s in range(SLICES - 1):
+        for s in range(last):
             features(s)
-            if s + 3 < SLICES:
-                if s + 3 != PACK:
-                    first_product(s + 3, 0)
-                if turned(s + 3, 1) and s + 3 != PACK:
-                    hold_d(s + 3)
-                    add_tide_turned(s + 3)
+            if s + 3 < SLICES and s + 3 != PACK:
+                first_product(s + 3, 0)
+                add_tide_turned(s + 3)
             if s == 0:
-                round_w1(*late_w1[0], nc.scalar.copy)
-                round_w1(*late_w1[1], nc.scalar.copy)
+                for a in range(PASSES):
+                    round_w1(1, a, 0, nc.scalar.copy)
             if s + 2 < SLICES:
                 add_tide(s + 2, 0)
                 if not turned(s + 2, 1):
@@ -303,47 +323,42 @@ def tile_list_tuna_dive_scores_kernel(
                 if turned(s + 2, 1):
                     turn_back(s + 2)
             if s == 1:
-                round_w1(*late_w1[2], nc.scalar.copy)
-                round_w1(*late_w1[3], nc.scalar.copy)
+                for a in range(PASSES):
+                    round_w1(1, a, 1, nc.scalar.copy)
             if s in (1, 2):
-                quantise_w1(*late_w1[2 * s - 2])
-                quantise_w1(*late_w1[2 * s - 1])
-            if s == 1:
+                for a in range(PASSES):
+                    quantise_w1(1, a, s - 1)
+            if s + 3 == PACK:
                 first_product(PACK, 1)
                 first_product(PACK, 0)
-                hold_d(PACK)
                 add_tide_turned(PACK)
-            if s >= 1 and s + 4 < SLICES:
+            if PACK < s + 4 < SLICES:
                 first_product(s + 4, 1)
-            if s == SLICES - 3:
+            if s == PACK:
                 interleave(0, 0, M // 2, nc.scalar.copy)
+            if s == PACK + 1:
                 interleave(0, M // 2, M, nc.scalar.copy)
+            if s == last - 1:
+                quantise_x(0, 0, M // 2)
+                open_sums(*first)
             pick(s, 0, 0, M)
             pick(s, 1, 0, M)
             add_picks(s, 0, M, nc.gpsimd)
-        last = SLICES - 1
-        first, second, third = PIECES
-
-        def open_sums(lo, hi):
-            for tiles in bank_tiles(lo, hi):
-                second_product(lo, hi, tiles, 0)
 
         features(last)
-        quantise_x(0, 0, M // 2)
-        open_sums(*first)
-        pick(last, 0, *first)
-        pick(last, 1, *first)
         quantise_x(0, M // 2, M)
         open_sums(*second)
         open_sums(*third)
-        add_picks(last, *first, nc.vector)
+        pick(last, 0, *first)
+        pick(last, 1, *first)
         pick(last, 0, *second)
-        interleave(1, *first, nc.vector.tensor_copy)
+        add_picks(last, *first, nc.vector)
+        interleave(1, *first, nc.scalar.copy)
         pick(last, 1, *second)
+        pick(last, 0, *third)
+        add_picks(last, *second, nc.vector)
         quantise_x(1, *first)
         scores(*first)
-        add_picks(last, *second, nc.vector)
-        pick(last, 0, *third)
         interleave(1, *second, nc.vector.tensor_copy)
         pick(last, 1, *third)
         quantise_x(1, *second)

import math
from contextlib import ExitStack

import concourse.mybir as mybir
from concourse.masks import make_identity

K, T, S, M, H, N = 1024, 4096, 1024, 512, 1024, 768
FLOPS = 2 * K * H * S + 2 * H * N * M

F32 = mybir.dt.float32
BF16 = mybir.dt.bfloat16
I32 = mybir.dt.int32
U32 = mybir.dt.uint32
U16 = mybir.dt.uint16
U8 = mybir.dt.uint8
FP8X4 = mybir.dt.float8_e4m3fn_x4
FP4X4 = mybir.dt.float4_e2m1fn_x4
ACT = mybir.ActivationFunctionType
ALU = mybir.AluOpType

P = 128
PACK = 4
PASS = P * PACK
PASSES = 2
QUADRANTS = 4
BANK = 512
SLICES = H // P
N_TILES = N // P
FIRST_TURNED = 3
BANKS = {"turned_sum": 2, "d_second": 1, "d_first": 3, "cosine": 2}
PIECES = ((0, 256), (256, 384), (384, 512))


def tile_list_tuna_dive_scores_kernel(
    tc, tab_words, tab_scales, offs, w1, tide, gain, offs2, offs3, wga, wgb, w4_words, w4_scales, out
):
    nc = tc.nc
    with ExitStack() as ctx:
        keep = ctx.enter_context(tc.tile_pool(name="keep", bufs=1))
        ring = ctx.enter_context(tc.tile_pool(name="ring", bufs=2))
        psum = ctx.enter_context(tc.psum_pool(name="psum", bufs=1))

        list1 = keep.tile([P, S // 16], U16, name="list1")
        list2 = keep.tile([P, M // 16], U16, name="list2")
        list3 = keep.tile([P, M // 16], U16, name="list3")
        words = [keep.tile([P, T], U32, name=f"words{a}") for a in range(PASSES)]
        tab_planes = keep.tile([P, T], U8, name="tab_planes")
        v_codes = [keep.tile([P, S], U32, name=f"v_codes{a}", align_bytes=64) for a in range(PASSES)]
        v_planes = keep.tile([P, S], U8, name="v_planes", align_bytes=64)
        w1_raw = {
            (b, a): keep.tile([P, PACK, PASS], F32, name=f"w1_raw{b}{a}") for b in range(PASSES) for a in range(PASSES)
        }
        tides = [keep.tile([P, S], F32, name=f"tide{s}", tag=f"tide{s}") for s in range(SLICES)]
        gains = keep.tile([P, PASSES, PACK], F32, name="gains")
        wa = keep.tile([P, M], F32, name="wa")
        wb = keep.tile([P, M], F32, name="wb")
        w4_codes = keep.tile([P, PASSES, 2 * N], U8, name="w4_codes", align_bytes=64)
        w4_planes = keep.tile([P, PASSES, N], U8, name="w4_planes", align_bytes=64)
        x_rows = [keep.tile([P, PACK, M], BF16, name=f"x_rows{b}") for b in range(PASSES)]

        identity = keep.tile([P, P], F32, name="identity")
        make_identity(nc, identity[:])

        def new_bank(role, shape=(P, BANK)):
            return psum.tile(list(shape), F32, name=role, tag=role, bufs=BANKS[role])


        def load_words(a):
            nc.sync.dma_start(
                out=words[a][:].bitcast(I32), in_=tab_words[a].rearrange("p t i -> p (t i)").bitcast(I32)
            )

        def load_w1(b, a):
            rows = w1[a * PASS : (a + 1) * PASS, b * PASS : (b + 1) * PASS]
            nc.sync.dma_start(out=w1_raw[b, a][:], in_=rows.rearrange("(p t) c -> p t c", t=PACK))

        tide_rows = tide.rearrange("(b p i) j -> b i p j", p=P, i=PACK)

        def load_tide(s):
            nc.sync.dma_start(out=tides[s][:], in_=tide_rows[s // PACK, s % PACK])

        nc.vector.memset(tab_planes[:].bitcast(I32), 0)
        nc.vector.memset(w4_planes[:].rearrange("p a n -> p (a n)").bitcast(I32), 0)

        warm = keep.tile([P, 1], F32, name="warm")
        nc.gpsimd.memset(warm[:], 0.0)
        nc.scalar.activation(warm[:], warm[:], ACT.Silu)

        nc.sync.dma_start(list1[:], offs)
        load_words(0)
        for q in range(QUADRANTS):
            nc.sync.dma_start(
                out=tab_planes[32 * q : 32 * q + 4 * PASSES, :].bitcast(I32),
                in_=tab_scales[:, 4 * q : 4 * q + 4, :].bitcast(I32),
            )
        load_words(1)
        load_w1(0, 0)
        load_w1(0, 1)
        load_tide(0)
        load_tide(1)
        nc.sync.dma_start(out=gains[:], in_=gain.rearrange("(b p i) -> p b i", p=P, i=PACK))
        nc.sync.dma_start(list2[:], offs2)
        nc.sync.dma_start(list3[:], offs3)
        load_tide(2)
        nc.sync.dma_start(out=wa[:], in_=wga)
        nc.sync.dma_start(out=wb[:], in_=wgb)
        load_w1(1, 0)
        load_w1(1, 1)
        for s in range(3, SLICES):
            load_tide(s)
        nc.sync.dma_start(out=w4_codes[:].bitcast(I32), in_=w4_words.rearrange("a p c -> p a c").bitcast(I32))
        for q in range(QUADRANTS):
            nc.sync.dma_start(
                out=w4_planes[32 * q : 32 * q + 4, :, :].bitcast(I32),
                in_=w4_scales[:, 4 * q : 4 * q + 4, :].rearrange("a r n -> r a n").bitcast(I32),
            )


        nc.vector.tensor_copy(v_codes[0][:], words[0][:].indirect(list1[:]))
        nc.vector.tensor_copy(v_planes[:], tab_planes[:].indirect(list1[:]))
        nc.vector.tensor_copy(v_codes[1][:], words[1][:].indirect(list1[:]))


        w1_bf, w1_codes, w1_planes = {}, {}, {}

        def round_w1(b, a, u, copy):
            rounded = ring.tile([P, 2 * PASS], BF16, name="w1_bf", tag="w1_bf", bufs=4, align_bytes=64)
            copy(
                rounded[:].rearrange("p (i m t) -> p m t i", i=2, t=PACK),
                w1_raw[b, a][:].rearrange("p t (m i) -> p m t i", i=PACK)[:, :, :, 2 * u : 2 * u + 2],
            )
            w1_bf[b, a, u] = rounded

        def quantise_w1(b, a, u):
            codes = keep.tile([P, 2 * P], U32, name=f"w1_codes{b}{a}{u}", align_bytes=64)
            planes = keep.tile([P, 2 * P], U8, name=f"w1_planes{b}{a}{u}", align_bytes=64)
            nc.vector.quantize_mx(out=codes[:].bitcast(FP8X4), scales=planes[:], in_=w1_bf[b, a, u][:])
            w1_codes[b, a, u] = codes
            w1_planes[b, a, u] = planes

        for a in range(PASSES):
            round_w1(0, a, 0, nc.vector.tensor_copy)
            round_w1(0, a, 1, nc.scalar.copy)
            quantise_w1(0, a, 0)
            quantise_w1(0, a, 1)


        d, z, c, h = {}, {}, {}, {}

        def turned(s, j):
            return j == 1 and s >= FIRST_TURNED

        def d_role(s, j):
            if j == 0:
                return "d_first"
            if turned(s, j):
                return "d_second"
            return "cosine" if s < BANKS["cosine"] else "turned_sum"

        def first_product(s, j):
            b, i = divmod(s, PACK)
            u, e = divmod(i, 2)
            cols = slice(e * P, (e + 1) * P)
            bank = new_bank(d_role(s, j))
            for a in range(PASSES):
                nc.tensor.matmul_mx(
                    out=bank[:],
                    lhsT=w1_codes[b, a, u][:, cols].bitcast(FP8X4),
                    lhsT_scale=w1_planes[b, a, u][:, cols],
                    rhs=v_codes[a][:, j * BANK : (j + 1) * BANK].bitcast(FP8X4),
                    rhs_scale=v_planes[4 * a : P, j * BANK : (j + 1) * BANK],
                    start=(a == 0),
                    stop=(a == PASSES - 1),
                )
            d[s, j] = bank

        def new_cosine_tile():
            return ring.tile([P, BANK], F32, name="c", tag="c", bufs=6)

        def add_tide(s, j):
            z[s, j] = new_cosine_tile()
            c[s, j] = z[s, j]
            nc.vector.tensor_tensor(z[s, j][:], tides[s][:, j * BANK : (j + 1) * BANK], d[s, j][:], ALU.add)

        def add_tide_turned(s):
            held = ring.tile([P, BANK], F32, name="held", tag="held", bufs=4)
            nc.scalar.copy(held[:], d[s, 1][:])
            d[s, 1] = held
            z[s, 1] = new_bank("turned_sum")
            c[s, 1] = new_cosine_tile()
            for part, source in enumerate((tides[s][:, BANK:S], held[:])):
                for k in range(BANK // P):
                    nc.tensor.matmul(
                        z[s, 1][:, k * P : (k + 1) * P],
                        source[:, k * P : (k + 1) * P],
                        identity[:],
                        start=(part == 0 and k == 0),
                        stop=(part == 1 and k == BANK // P - 1),
                        is_transpose=True,
                    )

        def magnitude(s, j):
            nc.scalar.activation(c[s, j][:], z[s, j][:], ACT.Abs)

        def cosine(s, j):
            nc.scalar.activation(c[s, j][:], c[s, j][:], ACT.Sin, bias=math.pi / 2, scale=-1.0)

        def turn_back(s):
            bank = new_bank("cosine")
            for k in range(BANK // P):
                nc.tensor.transpose(bank[:, k * P : (k + 1) * P], c[s, 1][:, k * P : (k + 1) * P], identity[:])
            c[s, 1] = bank

        def features(s):
            b, i = divmod(s, PACK)
            h[s] = ring.tile([P, S], F32, name="h", tag="h")
            for j in range(2):
                in_sbuf, in_psum = (d[s, j], c[s, j]) if turned(s, j) else (c[s, j], d[s, j])
                nc.vector.scalar_tensor_tensor(
                    h[s][:, j * BANK : (j + 1) * BANK], in_sbuf[:], gains[:, b, i : i + 1], in_psum[:], ALU.mult, ALU.mult
                )

        picked = {}

        def pick(s, side, lo, hi):
            offsets, weights = ((list2, wa), (list3, wb))[side]
            if side == 0 and s + 2 < SLICES:
                result = keep.tile([P, hi - lo], F32, name="picked", tag=f"tide{s + 2}")
            else:
                result = ring.tile([P, hi - lo], F32, name="picked", tag="picked", bufs=4)
            nc.vector.tensor_tensor(
                result[:], h[s][:].indirect(offsets[:, lo // 16 : hi // 16]), weights[:, lo:hi], ALU.mult
            )
            picked[s, side, lo] = result

        def add_picks(s, lo, hi, engine):
            b, i = divmod(s, PACK)
            engine.tensor_tensor(x_rows[b][:, i, lo:hi], picked[s, 0, lo][:], picked[s, 1, lo][:], ALU.add)


        x_bf = {}
        x_codes = [keep.tile([P, M], U32, name=f"x_codes{b}", align_bytes=64) for b in range(PASSES)]
        x_planes = [keep.tile([P, M], U8, name=f"x_planes{b}", align_bytes=64) for b in range(PASSES)]

        def interleave(b, lo, hi, copy):
            woven = keep.tile([P, (hi - lo) * PACK], BF16, name=f"x_bf{b}_{lo}", align_bytes=64)
            copy(
                woven[:].rearrange("p (c e i) -> p c i e", e=4, i=PACK),
                x_rows[b][:, :, lo:hi].rearrange("p i (c e) -> p c i e", e=4),
            )
            x_bf[b, lo] = woven

        def quantise_x(b, lo, hi):
            nc.vector.quantize_mx(
                out=x_codes[b][:, lo:hi].bitcast(FP8X4), scales=x_planes[b][:, lo:hi], in_=x_bf[b, lo][:]
            )

        y = {}
        roles = [role for role, count in BANKS.items() for k in range(count)]

        def bank_tiles(lo, hi):
            per_bank = 2 if hi == M else BANK // (hi - lo)
            return [range(n0, min(n0 + per_bank, N_TILES)) for n0 in range(0, N_TILES, per_bank)]

        def second_product(lo, hi, tiles, b):
            if b == 0:
                y[lo, tiles[0]] = new_bank(roles[len(y)], (P, len(tiles), hi - lo))
            for n in tiles:
                nc.tensor.matmul_mx(
                    out=y[lo, tiles[0]][:, n - tiles[0], :],
                    lhsT=w4_codes[:, b, 2 * n * P : 2 * (n + 1) * P].bitcast(FP4X4),
                    lhsT_scale=w4_planes[:, b, n * P : (n + 1) * P],
                    rhs=x_codes[b][:, lo:hi].bitcast(FP8X4),
                    rhs_scale=x_planes[b][:, lo:hi],
                    start=(b == 0 and n == tiles[0]),
                    stop=(b == PASSES - 1 and n == tiles[-1]),
                )

        def open_sums(lo, hi):
            for tiles in bank_tiles(lo, hi):
                second_product(lo, hi, tiles, 0)

        out_tiles = out.rearrange("(n p) m -> p n m", p=P)

        def scores(lo, hi):
            for tiles in bank_tiles(lo, hi):
                result = keep.tile([P, len(tiles), hi - lo], F32, name=f"scores{lo}_{tiles[0]}")
                second_product(lo, hi, tiles, 1)
                nc.scalar.activation(result[:], y[lo, tiles[0]][:], ACT.Tanh)
                queue = nc.scalar if hi == M and tiles[-1] == N_TILES - 1 else nc.sync
                queue.dma_start(out=out_tiles[:, tiles[0] : tiles[-1] + 1, lo:hi], in_=result[:])


        first, second, third = PIECES
        last = SLICES - 1
        for s in range(2):
            for j in range(2):
                first_product(s, j)
        for s in range(2):
            for j in range(2):
                add_tide(s, j)
                magnitude(s, j)
                cosine(s, j)
        first_product(2, 0)
        first_product(2, 1)
        first_product(3, 1)
        for s in range(last):
            features(s)
            if s + 3 < SLICES and s + 3 != PACK:
                first_product(s + 3, 0)
                add_tide_turned(s + 3)
            if s == 0:
                for a in range(PASSES):
                    round_w1(1, a, 0, nc.scalar.copy)
            if s + 2 < SLICES:
                add_tide(s + 2, 0)
                if not turned(s + 2, 1):
                    add_tide(s + 2, 1)
                magnitude(s + 2, 1)
                magnitude(s + 2, 0)
                cosine(s + 2, 1)
                cosine(s + 2, 0)
                if turned(s + 2, 1):
                    turn_back(s + 2)
            if s == 1:
                for a in range(PASSES):
                    round_w1(1, a, 1, nc.scalar.copy)
            if s in (1, 2):
                for a in range(PASSES):
                    quantise_w1(1, a, s - 1)
            if s + 3 == PACK:
                first_product(PACK, 1)
                first_product(PACK, 0)
                add_tide_turned(PACK)
            if PACK < s + 4 < SLICES:
                first_product(s + 4, 1)
            if s == PACK:
                interleave(0, 0, M // 2, nc.scalar.copy)
            if s == PACK + 1:
                interleave(0, M // 2, M, nc.scalar.copy)
            if s == last - 1:
                quantise_x(0, 0, M // 2)
                open_sums(*first)
            pick(s, 0, 0, M)
            pick(s, 1, 0, M)
            add_picks(s, 0, M, nc.gpsimd)

        features(last)
        quantise_x(0, M // 2, M)
        open_sums(*second)
        open_sums(*third)
        pick(last, 0, *first)
        pick(last, 1, *first)
        pick(last, 0, *second)
        add_picks(last, *first, nc.vector)
        interleave(1, *first, nc.scalar.copy)
        pick(last, 1, *second)
        pick(last, 0, *third)
        add_picks(last, *second, nc.vector)
        quantise_x(1, *first)
        scores(*first)
        interleave(1, *second, nc.vector.tensor_copy)
        pick(last, 1, *third)
        quantise_x(1, *second)
        scores(*second)
        add_picks(last, *third, nc.vector)
        interleave(1, *third, nc.vector.tensor_copy)
        quantise_x(1, *third)
        scores(*third)
